import numpy as np
import ml_dtypes


def mxq(x, axis, fmt="e4m3"):
    dtype, down = {"e4m3": (ml_dtypes.float8_e4m3fn, 7), "e5m2": (ml_dtypes.float8_e5m2, 14)}[fmt]
    v = np.moveaxis(np.asarray(x, np.float32).astype(ml_dtypes.bfloat16).astype(np.float64), axis, -1)
    blocks = v.reshape(v.shape[:-1] + (-1, 32))
    amax = np.abs(blocks).max(-1, keepdims=True)
    byte = np.maximum(np.where(amax > 0, np.frexp(amax)[1] - 1 + 127, 0) - down, 1)
    scale = np.exp2(byte - 127.0)
    codes = (blocks / scale).astype(np.float32).astype(dtype).astype(np.float64)
    return np.moveaxis((codes * scale).reshape(v.shape), -1, axis)


WIDE = False


def mx_kscale(k):
    if not WIDE:
        return np.ones(k)
    levels = np.array([10, -10, 5, -5, 0])
    if k % 512:
        return np.exp2(np.random.permutation(np.resize(levels, k // 32))).repeat(32)
    a = np.empty((k // 512, 16))
    for p in range(k // 512):
        a[p, :8] = np.random.permutation(np.resize(levels, 8))
        for g in range(8):
            far = levels[np.abs(levels - a[p, g]) >= 10]
            a[p, g + 8] = far[np.random.randint(len(far))]
    return np.exp2(a.ravel()).repeat(32)


def f64(x):
    return np.asarray(x).astype(np.float64)


def striped(idx):
    return np.tile(idx.reshape(-1, 16).T, (8, 1)).astype(np.uint16)


def unstriped(offs):
    return offs[:16].T.reshape(-1).astype(np.int64)


def pack_weight(w):
    k, n = w.shape
    w = f64(np.asarray(w, np.float32).astype(ml_dtypes.bfloat16)).reshape(k // 32, 32, n)
    amax = np.abs(w).max(1)
    byte = np.clip(np.where(amax > 0, np.frexp(amax)[1] - 1 + 127 - 7, 1), 1, 254)
    scaled = (w * np.exp2(127.0 - byte)[:, None, :]).reshape(k, n).astype(np.float32)
    words = np.ascontiguousarray(scaled.reshape(k // 512, 128, 4, n).transpose(0, 1, 3, 2)).astype(ml_dtypes.float8_e4m3fn).view(np.uint8)
    return words, np.ascontiguousarray(byte.astype(np.uint8).reshape(k // 512, 16, n))


def unpack_weight(words, scales):
    g, p, n, _ = words.shape
    vals = np.ascontiguousarray(words).view(ml_dtypes.float8_e4m3fn).astype(np.float64) * np.repeat(np.exp2(scales.astype(np.float64) - 127.0), 8, axis=1)[..., None]
    return vals.transpose(0, 1, 3, 2).reshape(g * 512, n)

def planes(y):
    n, m = y.shape
    v = y.astype(np.float32).astype(ml_dtypes.bfloat16).astype(np.float64).reshape(n // 32, 32, m)
    top = np.abs(v).max(1)
    byte = np.clip(np.where(top > 0, np.frexp(top)[1] - 1 + 127 - 7, 1), 1, 254)
    codes = (v * np.exp2(127.0 - byte)[:, None, :]).reshape(n, m).astype(np.float32).astype(ml_dtypes.float8_e4m3fn).view(np.uint8)
    words = codes.reshape(n // 512, 128, 4, m).transpose(0, 1, 3, 2)
    return np.ascontiguousarray(words), np.ascontiguousarray(byte.astype(np.uint8).reshape(n // 512, 16, m))


K, T, S, N, H, W, G = 512, 2048, 512, 512, 512, 1024, 384


def setup_inputs():
    n = np.random.standard_normal
    s = mx_kscale(K)[:, None]
    u = mx_kscale(S)
    packed_xT = pack_weight(n((K, T)) * s)
    return {
        "x_words": packed_xT[0],
        "x_scales": packed_xT[1],
        "wa": (n((K, H)) / np.sqrt(K) / s).astype(np.float32),
        "wb": (n((K, N)) / np.sqrt(K) / s).astype(np.float32),
        "gt": (np.random.uniform(0.5, 1.5, (S, 1)) * u[:, None]).astype(np.float32),
        "gi": (np.random.uniform(0.5, 1.5, (S, 1)) / u[:, None]).astype(np.float32),
        "offs": striped(np.random.permutation(T)[:S]),
        "two": striped(np.random.permutation(T)[:S]),
        "n1": striped(np.random.randint(0, H, W)),
        "n2": striped(np.random.permutation(H)),
        "n3": striped(np.random.permutation(N)[:G]),
        "n4": striped(np.random.permutation(N)[:G]),
        "n5": striped(np.random.permutation(N)),
        "n6": striped(np.random.permutation(N)),
    }


def reference(x_words, x_scales, wa, wb, gt, gi, offs, two, n1, n2, n3, n4, n5, n6):
    xq = unpack_weight(x_words, x_scales)[:, unstriped(offs)]
    a = xq.T @ mxq(f64(wa), 0, "e4m3")
    mb = a[:, unstriped(n1)]
    mx = mb.reshape(S, H, 2).max(axis=2)
    st = a - mx
    z = f64(gt) * (np.maximum(st, st[:, unstriped(n2)]))
    x_two = unpack_weight(x_words, x_scales)[:, unstriped(two)]
    b = x_two.T @ mxq(f64(wb), 0, "e4m3")
    pa = b[:, unstriped(n4)]
    old = b[:, unstriped(n3)]
    ra = np.minimum(pa, old) - (0.5 * pa)
    ds = b.copy()
    ds[:, unstriped(n3)] = ra
    z2 = f64(gi) * ds
    cv = 0.0625 * ((mxq(z, 0, "e4m3").T @ mxq(z2, 0, "e4m3")))
    st2 = np.maximum(cv, cv[:, unstriped(n5)])
    out_0 = st2[:, unstriped(n6)] - (0.5 * cv)
    return (out_0,) + planes(out_0)

@@ -1,0 +1,313 @@
+from contextlib import ExitStack
+
+import concourse.mybir as mybir
+from concourse.masks import make_identity
+
+F32 = mybir.dt.float32
+BF16 = mybir.dt.bfloat16
+I32 = mybir.dt.int32
+U32 = mybir.dt.uint32
+U16 = mybir.dt.uint16
+U8 = mybir.dt.uint8
+FP8X4 = mybir.dt.float8_e4m3fn_x4
+ALU = mybir.AluOpType
+ACT = mybir.ActivationFunctionType
+
+P = 128
+LANES = 4
+K, T, S, N, H, W, G = 512, 2048, 512, 512, 512, 1024, 384
+FLOPS = 3 * 2 * 512 * 512 * 512
+SPARE = 32
+HALF = 256
+
+
+def tile_picked_mombghopmkminhopb_none_po_kernel(
+    tc, x_words, x_scales, wa, wb, gt, gi, offs, two, n1, n2, n3, n4, n5, n6, out_0, out_1, out_2
+):
+    nc = tc.nc
+    with ExitStack() as ctx:
+        lists = ctx.enter_context(tc.tile_pool(name="lists", bufs=1))
+        keep = ctx.enter_context(tc.tile_pool(name="keep", bufs=1))
+        psum = ctx.enter_context(tc.psum_pool(name="psum", bufs=1))
+
+        def load_list(src, name):
+            tile = lists.tile(list(src.shape), U16, name=name)
+            nc.sync.dma_start(tile[:], src)
+            return tile
+
+        def sb(shape, dtype, name, tag=None):
+            return keep.tile(shape, dtype, name=name, tag=tag or name, align_bytes=64)
+
+        def bank(tag, name):
+            return psum.tile([P, 512], F32, name=name, tag=tag, bufs=2 if tag == "ring" else 1)
+
+        xs_rows = sb([P, T], U8, "xs_rows")
+        for q in range(4):
+            nc.sync.dma_start(
+                xs_rows[32 * q : 32 * q + 4, :].bitcast(I32), x_scales[0, 4 * q : 4 * q + 4, :].bitcast(I32)
+            )
+        two_sb = load_list(two, "two_sb")
+        offs_sb = load_list(offs, "offs_sb")
+        wb_raw = sb([P, LANES, N], F32, "wb_raw")
+        nc.sync.dma_start(wb_raw[:], wb.rearrange("(p j) w -> p j w", j=LANES))
+        xw = sb([P, T], I32, "xw")
+        nc.sync.dma_start(xw[:], x_words[0].rearrange("p n t -> p (n t)").bitcast(I32))
+        n4_sb = load_list(n4, "n4_sb")
+        n3_sb = load_list(n3, "n3_sb")
+        wa_raw = sb([P, LANES, H], F32, "wa_raw")
+        nc.sync.dma_start(wa_raw[:], wa.rearrange("(p j) w -> p j w", j=LANES))
+        n1_sb = load_list(n1, "n1_sb")
+        n2_sb = load_list(n2, "n2_sb")
+        n5_sb = load_list(n5, "n5_sb")
+        n6_sb = load_list(n6, "n6_sb")
+        gate_rows = sb([P, P], F32, "gate_rows")
+        nc.gpsimd.memset(gate_rows[:], 0.0)
+        for row, src in ((0, gt), (LANES, gi)):
+            nc.gpsimd.dma_start(
+                gate_rows[row : row + LANES, :].rearrange("t (q r) -> t q r", r=8),
+                src.rearrange("(q t r) o -> t q (r o)", t=LANES, r=8),
+            )
+        xs = sb([P, T], U8, "xs")
+        nc.vector.memset(xs[:].bitcast(I32), 0)
+        for q in range(4):
+            rows = slice(32 * q, 32 * q + 4)
+            nc.vector.tensor_copy(xs[rows, :].bitcast(I32), xs_rows[rows, :].bitcast(I32))
+
+        ident = sb([P, P], F32, "ident")
+        make_identity(nc, ident[:])
+
+        a_win = [sb([P, H + SPARE], F32, f"a_win{t}") for t in range(LANES)]
+        ds_win = [sb([P, 2 * G], F32, f"ds_win{t}") for t in range(LANES)]
+        cv_win = [sb([P, N + SPARE], F32, f"cv_win{t}") for t in range(LANES)]
+        for t in range(LANES):
+            nc.gpsimd.memset(a_win[t][:, H:], 0.0)
+        for t in range(LANES):
+            nc.gpsimd.memset(ds_win[t][:, N:], 0.0)
+        for t in range(LANES):
+            nc.gpsimd.memset(cv_win[t][:, N:], 0.0)
+
+        def interleave(copy, dst, src, c0, c1):
+            copy(
+                dst[:, LANES * c0 : LANES * c1].rearrange("p (c i j) -> p c j i", i=4, j=LANES),
+                src[:, :, c0:c1].rearrange("p j (c i) -> p c j i", i=4),
+            )
+
+        def quantise(src, name):
+            codes = sb([P, 512], U32, name + "_codes")
+            scales = sb([P, 512], U8, name + "_scales")
+            nc.vector.quantize_mx(out=codes[:].bitcast(FP8X4), scales=scales[:], in_=src[:])
+            return codes, scales
+
+        def pick_bytes(idx, name):
+            plain = sb([P, S], U8, name + "_plain")
+            nc.vector.tensor_copy(plain[:], xs[:].indirect(idx[:]))
+            dealt = sb([P, S], U8, name + "_dealt")
+            nc.vector.tensor_copy(
+                dealt[:].bitcast(I32).rearrange("p (t q r) -> p q t r", t=LANES, r=2),
+                plain[:].bitcast(I32).rearrange("p (q t r) -> p q t r", t=LANES, r=2),
+            )
+            return dealt
+
+        def pick_words(idx, name):
+            dealt = sb([P, S], U32, name)
+            nc.vector.tensor_copy(
+                dealt[:].rearrange("p (t q r) -> p q t r", t=LANES, r=8), xw[:].bitcast(U32).indirect(idx[:])
+            )
+            return dealt
+
+        def product(out, lhs, t, rhs):
+            cols = slice(P * t, P * (t + 1))
+            nc.tensor.matmul_mx(
+                out=out[:],
+                lhsT=lhs[0][:, cols].bitcast(FP8X4),
+                lhsT_scale=lhs[1][:, cols],
+                rhs=rhs[0][:].bitcast(FP8X4),
+                rhs_scale=rhs[1][:],
+                start=True,
+                stop=True,
+            )
+
+        gate_ps = bank("gate", "gate_ps")
+        nc.tensor.transpose(gate_ps[:, 0:P], gate_rows[:], ident[:])
+        gt_abs = sb([P, LANES], F32, "gt_abs")
+        nc.scalar.activation(gt_abs[:], gate_ps[:, 0:LANES], ACT.Abs)
+        gt_step = sb([P, LANES], F32, "gt_step")
+        nc.vector.tensor_scalar(gt_step[:], gate_ps[:, 0:LANES], 0.0, 2.0, ALU.is_ge, ALU.mult)
+        gi_signed = sb([P, LANES], F32, "gi_signed")
+        nc.vector.scalar_tensor_tensor(
+            gi_signed[:], gt_step[:], -1.0, gate_ps[:, LANES : 2 * LANES], ALU.add, ALU.mult
+        )
+
+        xb_scales = pick_bytes(two_sb, "xb_scales")
+        wb_bf = sb([P, LANES * N], BF16, "wb_bf")
+        interleave(nc.scalar.copy, wb_bf, wb_raw, 128, N)
+        interleave(nc.vector.tensor_copy, wb_bf, wb_raw, 0, 128)
+        xa_scales = pick_bytes(offs_sb, "xa_scales")
+        wb_q = quantise(wb_bf, "wb")
+        xb = (pick_words(two_sb, "xb_words"), xb_scales)
+        xa = (pick_words(offs_sb, "xa_words"), xa_scales)
+        wa_bf = sb([P, LANES * H], BF16, "wa_bf", "wa_bf_then_low0")
+        interleave(nc.vector.tensor_copy, wa_bf, wa_raw, 0, H)
+        wa_q = quantise(wa_bf, "wa")
+
+        st = sb([P, LANES * H], F32, "st")
+        z2_rows = sb([P, LANES, N], BF16, "z2_rows")
+
+        def a_load(t):
+            a_ps = bank("ring", f"a_ps{t}")
+            product(a_ps, xa, t, wa_q)
+            nc.scalar.activation(a_win[t][:, 0:H], a_ps[:], ACT.Copy, scale=gt_abs[:, t : t + 1])
+
+        def a_members(t):
+            mx = sb([P, H], F32, f"mx{t}", "mx3_then_st_n2" if t == 3 else None)
+            for h in range(2):
+                mb = sb([P, H], F32, f"mb{t}_{h}", "mb3_0_then_st_n2" if (t, h) == (3, 0) else None)
+                nc.scalar.activation(mb[:], a_win[t][:].indirect(n1_sb[:, 32 * h : 32 * (h + 1)]), ACT.Copy)
+                pairs = mb[:].rearrange("p (j m) -> p j m", m=2)
+                nc.vector.tensor_tensor(mx[:, HALF * h : HALF * (h + 1)], pairs[:, :, 0], pairs[:, :, 1], ALU.max)
+            nc.vector.tensor_tensor(st[:, H * t : H * (t + 1)], a_win[t][:, 0:H], mx[:], ALU.subtract)
+
+        def a_partner(t, h):
+            nc.scalar.activation(
+                st_n2[h][:, t, :],
+                st[:, H * t : H * (t + 1)].indirect(n2_sb[:, 16 * h : 16 * (h + 1)]),
+                ACT.Copy,
+            )
+
+        def b_load(t, copy):
+            b_ps = bank("ring", f"b_ps{t}")
+            product(b_ps, xb, t, wb_q)
+            copy(ds_win[t][:, 0:N], b_ps[:])
+
+        def b_path(t, old_on_vector):
+            less = sb([P, G], F32, f"less{t}")
+            nc.scalar.activation(less[:], ds_win[t][:].indirect(n4_sb[:]), ACT.Copy, scale=-0.5)
+            old = sb([P, G], F32, f"old{t}")
+            if old_on_vector:
+                nc.vector.tensor_copy(old[:], ds_win[t][:].indirect(n3_sb[:]))
+            else:
+                nc.scalar.activation(old[:], ds_win[t][:].indirect(n3_sb[:]), ACT.Copy)
+            low = sb([P, G], F32, f"low{t}", "wa_bf_then_low0")
+            nc.vector.scalar_tensor_tensor(low[:], less[:], -2.0, old[:], ALU.mult, ALU.min)
+            nc.vector.tensor_tensor(ds_win[t][:].indirect(n3_sb[:]), low[:], less[:], ALU.add)
+
+        def b_weigh(t, on_vector=True):
+            if on_vector:
+                nc.vector.tensor_scalar(z2_rows[:, t, :], ds_win[t][:, 0:N], gi_signed[:, t : t + 1], None, ALU.mult)
+            else:
+                nc.scalar.activation(z2_rows[:, t, :], ds_win[t][:, 0:N], ACT.Copy, scale=gi_signed[:, t : t + 1])
+
+        b_load(0, nc.scalar.copy)
+        b_load(1, nc.scalar.copy)
+        b_path(0, False)
+        b_path(1, False)
+        b_weigh(0)
+        a_load(0)
+        b_load(2, nc.scalar.copy)
+        b_weigh(1)
+        a_members(0)
+        b_path(2, False)
+        a_load(1)
+        b_load(3, nc.scalar.copy)
+        b_weigh(2)
+        a_members(1)
+        b_path(3, False)
+        a_load(2)
+        a_load(3)
+        b_weigh(3)
+        a_members(2)
+        a_members(3)
+        z2_bf = sb([P, LANES * N], BF16, "z2_bf", "a_win3")
+        interleave(nc.vector.tensor_copy, z2_bf, z2_rows, 0, N)
+        z2_q = quantise(z2_bf, "z2")
+        st_n2 = [sb([P, LANES, HALF], F32, f"st_n2_{h}", ("mb3_0_then_st_n2", "mx3_then_st_n2")[h]) for h in range(2)]
+
+        z_bf = sb([P, LANES * H], BF16, "z_bf")
+        for h in range(2):
+            for t in range(LANES):
+                a_partner(t, h)
+            ms = slice(64 * h, 64 * (h + 1))
+            nc.vector.tensor_tensor(
+                z_bf[:].rearrange("p (u m j) -> p m j u", u=LANES, j=LANES)[:, ms],
+                st[:].rearrange("p (j m u) -> p m j u", j=LANES, u=LANES)[:, ms],
+                st_n2[h][:].rearrange("p j (m u) -> p m j u", u=LANES),
+                ALU.max,
+            )
+        z_codes = sb([P, 512], U32, "z_codes")
+        z_scales = sb([P, 512], U8, "z_scales")
+        z_q = (z_codes, z_scales)
+
+        y = sb([P, LANES, N], F32, "y")
+        y_rows = out_0.rearrange("(p u) n -> p u n", u=LANES)
+        cv_ps = []
+        for u in range(LANES):
+            cols = slice(P * u, P * (u + 1))
+            nc.vector.quantize_mx(
+                out=z_codes[:, cols].bitcast(FP8X4), scales=z_scales[:, cols], in_=z_bf[:, 512 * u : 512 * (u + 1)]
+            )
+            cv_ps.append(bank(f"cv{u}", f"cv_ps{u}"))
+            product(cv_ps[u], z_q, u, z2_q)
+
+        st2 = [sb([P, N], F32, f"st2_{u}") for u in range(LANES)]
+
+        def cv_load(u, on_vector):
+            if on_vector:
+                nc.vector.tensor_scalar(cv_win[u][:, 0:N], cv_ps[u][:], -0.03125, None, ALU.mult)
+            else:
+                nc.scalar.activation(cv_win[u][:, 0:N], cv_ps[u][:], ACT.Copy, scale=-0.03125)
+
+        def cv_partner(u):
+            cv_n5 = sb([P, N], F32, f"cv_n5_{u}")
+            nc.scalar.activation(cv_n5[:], cv_win[u][:].indirect(n5_sb[:]), ACT.Copy, scale=-2.0)
+            nc.vector.scalar_tensor_tensor(st2[u][:], cv_ps[u][:], 0.0625, cv_n5[:], ALU.mult, ALU.max)
+
+        def finish(u, h, on_vector):
+            cols = slice(HALF * h, HALF * (h + 1))
+            picked = st2[u][:].indirect(n6_sb[:, 16 * h : 16 * (h + 1)])
+            if not on_vector:
+                plain = sb([P, HALF], F32, f"st2_n6_{u}_{h}")
+                nc.scalar.activation(plain[:], picked, ACT.Copy)
+                picked = plain[:]
+            nc.vector.tensor_tensor(y[:, u, cols], picked, cv_win[u][:, cols], ALU.add)
+
+        y_bf = sb([P, LANES * N], BF16, "y_bf")
+        y_codes = sb([P, N], U32, "y_codes")
+        y_scales = sb([P, N], U8, "y_scales")
+        words_out = out_1[0].rearrange("p n t -> p (n t)").bitcast(I32)
+
+        def planes(h, copy):
+            cols = slice(HALF * h, HALF * (h + 1))
+            interleave(copy, y_bf, y, HALF * h, HALF * (h + 1))
+            nc.vector.quantize_mx(
+                out=y_codes[:, cols].bitcast(FP8X4),
+                scales=y_scales[:, cols],
+                in_=y_bf[:, LANES * HALF * h : LANES * HALF * (h + 1)],
+            )
+            nc.sync.dma_start(words_out[:, cols], y_codes[:, cols].bitcast(I32))
+
+        cv_load(0, False)
+        cv_load(1, True)
+        cv_load(2, True)
+        cv_partner(0)
+        finish(0, 0, True)
+        cv_partner(1)
+        finish(1, 0, True)
+        finish(0, 1, True)
+        nc.sync.dma_start(y_rows[:, 0, :], y[:, 0, :])
+        cv_partner(2)
+        cv_load(3, False)
+        finish(2, 0, True)
+        cv_partner(3)
+        finish(1, 1, False)
+        nc.sync.dma_start(y_rows[:, 1, :], y[:, 1, :])
+        finish(3, 0, True)
+        finish(2, 1, False)
+        nc.sync.dma_start(y_rows[:, 2, :], y[:, 2, :])
+        finish(3, 1, True)
+        nc.sync.dma_start(y_rows[:, 3, :], y[:, 3, :])
+        planes(0, nc.scalar.copy)
+        planes(1, nc.vector.tensor_copy)
+        for q in range(4):
+            nc.sync.dma_start(
+                out_2[0, 4 * q : 4 * q + 4, :].bitcast(I32), y_scales[32 * q : 32 * q + 4, :].bitcast(I32)
+            )

@@ -56,23 +56,19 @@ def tile_picked_mombghopmkminhopb_none_po_kernel(
         n3_sb = load_list(n3, "n3_sb")
         wa_raw = sb([P, LANES, H], F32, "wa_raw")
         nc.sync.dma_start(wa_raw[:], wa.rearrange("(p j) w -> p j w", j=LANES))
+        gate_rows = sb([P, P], F32, "gate_rows")
+        nc.gpsimd.memset(gate_rows[:], 0.0)
+        for row, src in ((0, gt), (LANES, gi)):
+            nc.sync.dma_start(
+                gate_rows[row : row + LANES, :].rearrange("t (q r) -> t q r", r=8),
+                src.rearrange("(q t r) o -> t q (r o)", t=LANES, r=8),
+            )
         n1_sb = load_list(n1, "n1_sb")
         n2_sb = load_list(n2, "n2_sb")
         n5_sb = load_list(n5, "n5_sb")
         n6_sb = load_list(n6, "n6_sb")
-        gate_rows = sb([P, P], F32, "gate_rows")
-        nc.gpsimd.memset(gate_rows[:], 0.0)
-        for row, src in ((0, gt), (LANES, gi)):
-            nc.gpsimd.dma_start(
-                gate_rows[row : row + LANES, :].rearrange("t (q r) -> t q r", r=8),
-                src.rearrange("(q t r) o -> t q (r o)", t=LANES, r=8),
-            )
         xs = sb([P, T], U8, "xs")
         nc.vector.memset(xs[:].bitcast(I32), 0)
-        for q in range(4):
-            rows = slice(32 * q, 32 * q + 4)
-            nc.vector.tensor_copy(xs[rows, :].bitcast(I32), xs_rows[rows, :].bitcast(I32))
-
         ident = sb([P, P], F32, "ident")
         make_identity(nc, ident[:])
 
@@ -80,11 +76,15 @@ def tile_picked_mombghopmkminhopb_none_po_kernel(
         ds_win = [sb([P, 2 * G], F32, f"ds_win{t}") for t in range(LANES)]
         cv_win = [sb([P, N + SPARE], F32, f"cv_win{t}") for t in range(LANES)]
         for t in range(LANES):
-            nc.gpsimd.memset(a_win[t][:, H:], 0.0)
+            nc.vector.memset(a_win[t][:, H:], 0.0)
         for t in range(LANES):
-            nc.gpsimd.memset(ds_win[t][:, N:], 0.0)
+            nc.vector.memset(ds_win[t][:, N:], 0.0)
         for t in range(LANES):
-            nc.gpsimd.memset(cv_win[t][:, N:], 0.0)
+            nc.vector.memset(cv_win[t][:, N:], 0.0)
+
+        for q in range(4):
+            rows = slice(32 * q, 32 * q + 4)
+            nc.vector.tensor_copy(xs[rows, :].bitcast(I32), xs_rows[rows, :].bitcast(I32))
 
         def interleave(copy, dst, src, c0, c1):
             copy(
@@ -127,23 +127,13 @@ def tile_picked_mombghopmkminhopb_none_po_kernel(
                 stop=True,
             )
 
-        gate_ps = bank("gate", "gate_ps")
-        nc.tensor.transpose(gate_ps[:, 0:P], gate_rows[:], ident[:])
-        gt_abs = sb([P, LANES], F32, "gt_abs")
-        nc.scalar.activation(gt_abs[:], gate_ps[:, 0:LANES], ACT.Abs)
-        gt_step = sb([P, LANES], F32, "gt_step")
-        nc.vector.tensor_scalar(gt_step[:], gate_ps[:, 0:LANES], 0.0, 2.0, ALU.is_ge, ALU.mult)
-        gi_signed = sb([P, LANES], F32, "gi_signed")
-        nc.vector.scalar_tensor_tensor(
-            gi_signed[:], gt_step[:], -1.0, gate_ps[:, LANES : 2 * LANES], ALU.add, ALU.mult
-        )
-
         xb_scales = pick_bytes(two_sb, "xb_scales")
-        wb_bf = sb([P, LANES * N], BF16, "wb_bf")
-        interleave(nc.scalar.copy, wb_bf, wb_raw, 128, N)
-        interleave(nc.vector.tensor_copy, wb_bf, wb_raw, 0, 128)
         xa_scales = pick_bytes(offs_sb, "xa_scales")
-        wb_q = quantise(wb_bf, "wb")
+        wb_q = (sb([P, N], U32, "wb_codes"), sb([P, N], U8, "wb_scales"))
+        for copy, c0, c1, tag in ((nc.vector.tensor_copy, 0, 128, "xb_words"), (nc.scalar.copy, 128, N, "xa_words")):
+            part = sb([P, LANES * (c1 - c0)], BF16, f"wb_bf{c0}", tag)
+            interleave(copy, part, wb_raw[:, :, c0:c1], 0, c1 - c0)
+            nc.vector.quantize_mx(out=wb_q[0][:, c0:c1].bitcast(FP8X4), scales=wb_q[1][:, c0:c1], in_=part[:])
         xb = (pick_words(two_sb, "xb_words"), xb_scales)
         xa = (pick_words(offs_sb, "xa_words"), xa_scales)
         wa_bf = sb([P, LANES * H], BF16, "wa_bf", "wa_bf_then_low0")
@@ -156,7 +146,10 @@ def tile_picked_mombghopmkminhopb_none_po_kernel(
         def a_load(t):
             a_ps = bank("ring", f"a_ps{t}")
             product(a_ps, xa, t, wa_q)
-            nc.scalar.activation(a_win[t][:, 0:H], a_ps[:], ACT.Copy, scale=gt_abs[:, t : t + 1])
+            if t in ():
+                nc.vector.tensor_scalar(a_win[t][:, 0:H], a_ps[:], gt_abs[:, t : t + 1], None, ALU.mult)
+            else:
+                nc.scalar.activation(a_win[t][:, 0:H], a_ps[:], ACT.Copy, scale=gt_abs[:, t : t + 1])
 
         def a_members(t):
             mx = sb([P, H], F32, f"mx{t}", "mx3_then_st_n2" if t == 3 else None)
@@ -168,14 +161,14 @@ def tile_picked_mombghopmkminhopb_none_po_kernel(
             nc.vector.tensor_tensor(st[:, H * t : H * (t + 1)], a_win[t][:, 0:H], mx[:], ALU.subtract)
 
         def a_partner(t, h):
-            nc.scalar.activation(
-                st_n2[h][:, t, :],
-                st[:, H * t : H * (t + 1)].indirect(n2_sb[:, 16 * h : 16 * (h + 1)]),
-                ACT.Copy,
-            )
+            picked = st[:, H * t : H * (t + 1)].indirect(n2_sb[:, 16 * h : 16 * (h + 1)])
+            if (t, h) in ((3, 0), (3, 1)):
+                nc.vector.tensor_copy(st_n2[h][:, t, :], picked)
+            else:
+                nc.scalar.activation(st_n2[h][:, t, :], picked, ACT.Copy)
 
         def b_load(t, copy):
-            b_ps = bank("ring", f"b_ps{t}")
+            b_ps = bank("ring" if t else "first", f"b_ps{t}")
             product(b_ps, xb, t, wb_q)
             copy(ds_win[t][:, 0:N], b_ps[:])
 
@@ -199,6 +192,17 @@ def tile_picked_mombghopmkminhopb_none_po_kernel(
 
         b_load(0, nc.scalar.copy)
         b_load(1, nc.scalar.copy)
+        gate_ps = bank("first", "gate_ps")
+        nc.tensor.transpose(gate_ps[:, 0:P], gate_rows[:], ident[:])
+        gt_step = sb([P, LANES], F32, "gt_step")
+        nc.vector.tensor_scalar(gt_step[:], gate_ps[:, 0:LANES], 0.0, 2.0, ALU.is_ge, ALU.mult)
+        gt_abs = sb([P, LANES], F32, "gt_abs")
+        nc.vector.scalar_tensor_tensor(gt_abs[:], gt_step[:], -1.0, gate_ps[:, 0:LANES], ALU.add, ALU.mult)
+        gi_signed = sb([P, LANES], F32, "gi_signed")
+        nc.vector.scalar_tensor_tensor(
+            gi_signed[:], gt_step[:], -1.0, gate_ps[:, LANES : 2 * LANES], ALU.add, ALU.mult
+        )
+
         b_path(0, False)
         b_path(1, False)
         b_weigh(0)
@@ -217,7 +221,7 @@ def tile_picked_mombghopmkminhopb_none_po_kernel(
         b_weigh(3)
         a_members(2)
         a_members(3)
-        z2_bf = sb([P, LANES * N], BF16, "z2_bf", "a_win3")
+        z2_bf = sb([P, LANES * N], BF16, "z2_bf")
         interleave(nc.vector.tensor_copy, z2_bf, z2_rows, 0, N)
         z2_q = quantise(z2_bf, "z2")
         st_n2 = [sb([P, LANES, HALF], F32, f"st_n2_{h}", ("mb3_0_then_st_n2", "mx3_then_st_n2")[h]) for h in range(2)]
@@ -237,7 +241,7 @@ def tile_picked_mombghopmkminhopb_none_po_kernel(
         z_scales = sb([P, 512], U8, "z_scales")
         z_q = (z_codes, z_scales)
 
-        y = sb([P, LANES, N], F32, "y")
+        y = [sb([P, LANES, HALF], F32, f"y{h}") for h in range(2)]
         y_rows = out_0.rearrange("(p u) n -> p u n", u=LANES)
         cv_ps = []
         for u in range(LANES):
@@ -261,53 +265,54 @@ def tile_picked_mombghopmkminhopb_none_po_kernel(
             nc.scalar.activation(cv_n5[:], cv_win[u][:].indirect(n5_sb[:]), ACT.Copy, scale=-2.0)
             nc.vector.scalar_tensor_tensor(st2[u][:], cv_ps[u][:], 0.0625, cv_n5[:], ALU.mult, ALU.max)
 
-        def finish(u, h, on_vector):
+        def finish(u, h, how):
+            adder = nc.gpsimd if how in ("sg", "vg") else nc.vector
             cols = slice(HALF * h, HALF * (h + 1))
             picked = st2[u][:].indirect(n6_sb[:, 16 * h : 16 * (h + 1)])
-            if not on_vector:
+            if how != "fused":
                 plain = sb([P, HALF], F32, f"st2_n6_{u}_{h}")
-                nc.scalar.activation(plain[:], picked, ACT.Copy)
+                if how in ("s", "sg"):
+                    nc.scalar.activation(plain[:], picked, ACT.Copy)
+                else:
+                    nc.vector.tensor_copy(plain[:], picked)
                 picked = plain[:]
-            nc.vector.tensor_tensor(y[:, u, cols], picked, cv_win[u][:, cols], ALU.add)
+            adder.tensor_tensor(y[h][:, u, :], picked, cv_win[u][:, cols], ALU.add)
+            store(u, h)
 
-        y_bf = sb([P, LANES * N], BF16, "y_bf")
+        y_bf = [sb([P, LANES * HALF], BF16, f"y_bf{h}") for h in range(2)]
         y_codes = sb([P, N], U32, "y_codes")
         y_scales = sb([P, N], U8, "y_scales")
         words_out = out_1[0].rearrange("p n t -> p (n t)").bitcast(I32)
 
-        def planes(h, copy):
+        def planes(h, shares):
             cols = slice(HALF * h, HALF * (h + 1))
-            interleave(copy, y_bf, y, HALF * h, HALF * (h + 1))
-            nc.vector.quantize_mx(
-                out=y_codes[:, cols].bitcast(FP8X4),
-                scales=y_scales[:, cols],
-                in_=y_bf[:, LANES * HALF * h : LANES * HALF * (h + 1)],
-            )
+            for copy, c0, c1 in shares:
+                interleave(copy, y_bf[h], y[h], c0, c1)
+            nc.vector.quantize_mx(out=y_codes[:, cols].bitcast(FP8X4), scales=y_scales[:, cols], in_=y_bf[h][:])
             nc.sync.dma_start(words_out[:, cols], y_codes[:, cols].bitcast(I32))
+
+        def store(u, h):
+            nc.sync.dma_start(y_rows[:, u, HALF * h : HALF * (h + 1)], y[h][:, u, :])
 
         cv_load(0, False)
         cv_load(1, True)
         cv_load(2, True)
+        cv_load(3, True)
         cv_partner(0)
-        finish(0, 0, True)
+        finish(0, 0, "fused")
         cv_partner(1)
-        finish(1, 0, True)
-        finish(0, 1, True)
-        nc.sync.dma_start(y_rows[:, 0, :], y[:, 0, :])
+        finish(1, 0, "fused")
         cv_partner(2)
-        cv_load(3, False)
-        finish(2, 0, True)
+        finish(0, 1, "fused")
         cv_partner(3)
-        finish(1, 1, False)
-        nc.sync.dma_start(y_rows[:, 1, :], y[:, 1, :])
-        finish(3, 0, True)
-        finish(2, 1, False)
-        nc.sync.dma_start(y_rows[:, 2, :], y[:, 2, :])
-        finish(3, 1, True)
-        nc.sync.dma_start(y_rows[:, 3, :], y[:, 3, :])
-        planes(0, nc.scalar.copy)
-        planes(1, nc.vector.tensor_copy)
+        finish(2, 0, "s")
+        finish(3, 0, "s")
+        finish(1, 1, "fused")
+        finish(2, 1, "s")
+        planes(0, ((nc.scalar.copy, 0, HALF),))
+        finish(3, 1, "fused")
+        planes(1, ((nc.scalar.copy, 0, 96), (nc.vector.tensor_copy, 96, HALF)))
         for q in range(4):
-            nc.sync.dma_start(
+            (nc.sync, nc.scalar)[q % 2].dma_start(
                 out_2[0, 4 * q : 4 * q + 4, :].bitcast(I32), y_scales[32 * q : 32 * q + 4, :].bitcast(I32)
             )

@@ -19,6 +19,7 @@ K, T, S, N, H, W, G = 512, 2048, 512, 512, 512, 1024, 384
 FLOPS = 3 * 2 * 512 * 512 * 512
 SPARE = 32
 HALF = 256
+PIECES = ((0, 256), (256, 384), (384, 512))
 
 
 def tile_picked_mombghopmkminhopb_none_po_kernel(
@@ -129,14 +130,12 @@ def tile_picked_mombghopmkminhopb_none_po_kernel(
 
         xb_scales = pick_bytes(two_sb, "xb_scales")
         xa_scales = pick_bytes(offs_sb, "xa_scales")
-        wb_q = (sb([P, N], U32, "wb_codes"), sb([P, N], U8, "wb_scales"))
-        for copy, c0, c1, tag in ((nc.vector.tensor_copy, 0, 128, "xb_words"), (nc.scalar.copy, 128, N, "xa_words")):
-            part = sb([P, LANES * (c1 - c0)], BF16, f"wb_bf{c0}", tag)
-            interleave(copy, part, wb_raw[:, :, c0:c1], 0, c1 - c0)
-            nc.vector.quantize_mx(out=wb_q[0][:, c0:c1].bitcast(FP8X4), scales=wb_q[1][:, c0:c1], in_=part[:])
         xb = (pick_words(two_sb, "xb_words"), xb_scales)
+        wb_bf = sb([P, LANES * N], BF16, "wb_bf", "xa_words")
+        interleave(nc.scalar.copy, wb_bf, wb_raw, 0, N)
+        wb_q = quantise(wb_bf, "wb")
         xa = (pick_words(offs_sb, "xa_words"), xa_scales)
-        wa_bf = sb([P, LANES * H], BF16, "wa_bf", "wa_bf_then_low0")
+        wa_bf = sb([P, LANES * H], BF16, "wa_bf", "wa_bf_then_old0")
         interleave(nc.vector.tensor_copy, wa_bf, wa_raw, 0, H)
         wa_q = quantise(wa_bf, "wa")
 
@@ -151,17 +150,21 @@ def tile_picked_mombghopmkminhopb_none_po_kernel(
             else:
                 nc.scalar.activation(a_win[t][:, 0:H], a_ps[:], ACT.Copy, scale=gt_abs[:, t : t + 1])
 
-        def a_members(t):
-            mx = sb([P, H], F32, f"mx{t}", "mx3_then_st_n2" if t == 3 else None)
-            for h in range(2):
-                mb = sb([P, H], F32, f"mb{t}_{h}", "mb3_0_then_st_n2" if (t, h) == (3, 0) else None)
-                nc.scalar.activation(mb[:], a_win[t][:].indirect(n1_sb[:, 32 * h : 32 * (h + 1)]), ACT.Copy)
-                pairs = mb[:].rearrange("p (j m) -> p j m", m=2)
-                nc.vector.tensor_tensor(mx[:, HALF * h : HALF * (h + 1)], pairs[:, :, 0], pairs[:, :, 1], ALU.max)
-            nc.vector.tensor_tensor(st[:, H * t : H * (t + 1)], a_win[t][:, 0:H], mx[:], ALU.subtract)
+        mx = {}
+
+        def a_half(t, h):
+            if h == 0:
+                mx[t] = sb([P, H], F32, f"mx{t}", "mx3_then_st_n2" if t == 3 else None)
+            mb = sb([P, H], F32, f"mb{t}_{h}", f"mb3_{h}_then_st_n2" if t == 3 else None)
+            nc.scalar.activation(mb[:], a_win[t][:].indirect(n1_sb[:, 32 * h : 32 * (h + 1)]), ACT.Copy)
+            pairs = mb[:].rearrange("p (j m) -> p j m", m=2)
+            nc.vector.tensor_tensor(mx[t][:, HALF * h : HALF * (h + 1)], pairs[:, :, 0], pairs[:, :, 1], ALU.max)
+
+        def a_less(t):
+            nc.vector.tensor_tensor(st[:, H * t : H * (t + 1)], a_win[t][:, 0:H], mx[t][:], ALU.subtract)
 
         def a_partner(t, h):
-            picked = st[:, H * t : H * (t + 1)].indirect(n2_sb[:, 16 * h : 16 * (h + 1)])
+            picked = st[:, H * t : H * (t + 1)].indirect(n2_sb[:, PIECES[h][0] // 16 : PIECES[h][1] // 16])
             if (t, h) in ((3, 0), (3, 1)):
                 nc.vector.tensor_copy(st_n2[h][:, t, :], picked)
             else:
@@ -172,16 +175,26 @@ def tile_picked_mombghopmkminhopb_none_po_kernel(
             product(b_ps, xb, t, wb_q)
             copy(ds_win[t][:, 0:N], b_ps[:])
 
+        less_low = {}
+
         def b_path(t, old_on_vector):
+            b_pick(t, old_on_vector)
+            b_put(t)
+
+        def b_pick(t, old_on_vector=False):
             less = sb([P, G], F32, f"less{t}")
             nc.scalar.activation(less[:], ds_win[t][:].indirect(n4_sb[:]), ACT.Copy, scale=-0.5)
-            old = sb([P, G], F32, f"old{t}")
+            old = sb([P, G], F32, f"old{t}", "wa_bf_then_old0" if t == 0 else None)
             if old_on_vector:
                 nc.vector.tensor_copy(old[:], ds_win[t][:].indirect(n3_sb[:]))
             else:
                 nc.scalar.activation(old[:], ds_win[t][:].indirect(n3_sb[:]), ACT.Copy)
-            low = sb([P, G], F32, f"low{t}", "wa_bf_then_low0")
+            low = sb([P, G], F32, f"low{t}", "low01" if t < 2 else None)
             nc.vector.scalar_tensor_tensor(low[:], less[:], -2.0, old[:], ALU.mult, ALU.min)
+            less_low[t] = (less, low)
+
+        def b_put(t):
+            less, low = less_low[t]
             nc.vector.tensor_tensor(ds_win[t][:].indirect(n3_sb[:]), low[:], less[:], ALU.add)
 
         def b_weigh(t, on_vector=True):
@@ -203,38 +216,44 @@ def tile_picked_mombghopmkminhopb_none_po_kernel(
             gi_signed[:], gt_step[:], -1.0, gate_ps[:, LANES : 2 * LANES], ALU.add, ALU.mult
         )
 
-        b_path(0, False)
+        b_path(0, True)
         b_path(1, False)
         b_weigh(0)
-        a_load(0)
-        b_load(2, nc.scalar.copy)
-        b_weigh(1)
-        a_members(0)
-        b_path(2, False)
-        a_load(1)
-        b_load(3, nc.scalar.copy)
-        b_weigh(2)
-        a_members(1)
-        b_path(3, False)
+        for t in range(2):
+            a_load(t)
+            b_load(t + 2, nc.scalar.copy)
+            a_half(t, 0)
+            b_weigh(t + 1)
+            b_pick(t + 2)
+            a_half(t, 1)
+            b_put(t + 2)
+            a_less(t)
         a_load(2)
         a_load(3)
+        a_half(2, 0)
         b_weigh(3)
-        a_members(2)
-        a_members(3)
+        a_half(2, 1)
+        a_half(3, 0)
+        a_less(2)
+        a_half(3, 1)
         z2_bf = sb([P, LANES * N], BF16, "z2_bf")
         interleave(nc.vector.tensor_copy, z2_bf, z2_rows, 0, N)
+        a_less(3)
         z2_q = quantise(z2_bf, "z2")
-        st_n2 = [sb([P, LANES, HALF], F32, f"st_n2_{h}", ("mb3_0_then_st_n2", "mx3_then_st_n2")[h]) for h in range(2)]
+        st_n2 = [
+            sb([P, LANES, c1 - c0], F32, f"st_n2_{i}", ("mb3_0_then_st_n2", "mx3_then_st_n2", "a_win3", None)[i])
+            for i, (c0, c1) in enumerate(PIECES)
+        ]
 
         z_bf = sb([P, LANES * H], BF16, "z_bf")
-        for h in range(2):
+        for i, (c0, c1) in enumerate(PIECES):
             for t in range(LANES):
-                a_partner(t, h)
-            ms = slice(64 * h, 64 * (h + 1))
+                a_partner(t, i)
+            ms = slice(c0 // LANES, c1 // LANES)
             nc.vector.tensor_tensor(
                 z_bf[:].rearrange("p (u m j) -> p m j u", u=LANES, j=LANES)[:, ms],
                 st[:].rearrange("p (j m u) -> p m j u", j=LANES, u=LANES)[:, ms],
-                st_n2[h][:].rearrange("p j (m u) -> p m j u", u=LANES),
+                st_n2[i][:].rearrange("p j (m u) -> p m j u", u=LANES),
                 ALU.max,
             )
         z_codes = sb([P, 512], U32, "z_codes")
@@ -244,11 +263,11 @@ def tile_picked_mombghopmkminhopb_none_po_kernel(
         y = [sb([P, LANES, HALF], F32, f"y{h}") for h in range(2)]
         y_rows = out_0.rearrange("(p u) n -> p u n", u=LANES)
         cv_ps = []
-        for u in range(LANES):
-            cols = slice(P * u, P * (u + 1))
+        for c0, c1 in ((0, P), (P, H)):
             nc.vector.quantize_mx(
-                out=z_codes[:, cols].bitcast(FP8X4), scales=z_scales[:, cols], in_=z_bf[:, 512 * u : 512 * (u + 1)]
+                out=z_codes[:, c0:c1].bitcast(FP8X4), scales=z_scales[:, c0:c1], in_=z_bf[:, LANES * c0 : LANES * c1]
             )
+        for u in range(LANES):
             cv_ps.append(bank(f"cv{u}", f"cv_ps{u}"))
             product(cv_ps[u], z_q, u, z2_q)
 

from contextlib import ExitStack

import concourse.mybir as mybir
from concourse.masks import make_identity

F32 = mybir.dt.float32
BF16 = mybir.dt.bfloat16
I32 = mybir.dt.int32
U32 = mybir.dt.uint32
U16 = mybir.dt.uint16
U8 = mybir.dt.uint8
FP8X4 = mybir.dt.float8_e4m3fn_x4
ALU = mybir.AluOpType
ACT = mybir.ActivationFunctionType

P = 128
LANES = 4
K, T, S, N, H, W, G = 512, 2048, 512, 512, 512, 1024, 384
FLOPS = 3 * 2 * 512 * 512 * 512
SPARE = 32
HALF = 256
PIECES = ((0, 256), (256, 384), (384, 512))


def tile_picked_mombghopmkminhopb_none_po_kernel(
    tc, x_words, x_scales, wa, wb, gt, gi, offs, two, n1, n2, n3, n4, n5, n6, out_0, out_1, out_2
):
    nc = tc.nc
    with ExitStack() as ctx:
        lists = ctx.enter_context(tc.tile_pool(name="lists", bufs=1))
        keep = ctx.enter_context(tc.tile_pool(name="keep", bufs=1))
        psum = ctx.enter_context(tc.psum_pool(name="psum", bufs=1))

        def load_list(src, name):
            tile = lists.tile(list(src.shape), U16, name=name)
            nc.sync.dma_start(tile[:], src)
            return tile

        def sb(shape, dtype, name, tag=None):
            return keep.tile(shape, dtype, name=name, tag=tag or name, align_bytes=64)

        def bank(tag, name):
            return psum.tile([P, 512], F32, name=name, tag=tag, bufs=2 if tag == "ring" else 1)

        xs_rows = sb([P, T], U8, "xs_rows")
        for q in range(4):
            nc.sync.dma_start(
                xs_rows[32 * q : 32 * q + 4, :].bitcast(I32), x_scales[0, 4 * q : 4 * q + 4, :].bitcast(I32)
            )
        two_sb = load_list(two, "two_sb")
        offs_sb = load_list(offs, "offs_sb")
        wb_raw = sb([P, LANES, N], F32, "wb_raw")
        nc.sync.dma_start(wb_raw[:], wb.rearrange("(p j) w -> p j w", j=LANES))
        xw = sb([P, T], I32, "xw")
        nc.sync.dma_start(xw[:], x_words[0].rearrange("p n t -> p (n t)").bitcast(I32))
        n4_sb = load_list(n4, "n4_sb")
        n3_sb = load_list(n3, "n3_sb")
        wa_raw = sb([P, LANES, H], F32, "wa_raw")
        nc.sync.dma_start(wa_raw[:], wa.rearrange("(p j) w -> p j w", j=LANES))
        gate_rows = sb([P, P], F32, "gate_rows")
        nc.gpsimd.memset(gate_rows[:], 0.0)
        for row, src in ((0, gt), (LANES, gi)):
            nc.sync.dma_start(
                gate_rows[row : row + LANES, :].rearrange("t (q r) -> t q r", r=8),
                src.rearrange("(q t r) o -> t q (r o)", t=LANES, r=8),
            )
        n1_sb = load_list(n1, "n1_sb")
        n2_sb = load_list(n2, "n2_sb")
        n5_sb = load_list(n5, "n5_sb")
        n6_sb = load_list(n6, "n6_sb")
        xs = sb([P, T], U8, "xs")
        nc.vector.memset(xs[:].bitcast(I32), 0)
        ident = sb([P, P], F32, "ident")
        make_identity(nc, ident[:])

        a_win = [sb([P, H + SPARE], F32, f"a_win{t}") for t in range(LANES)]
        ds_win = [sb([P, 2 * G], F32, f"ds_win{t}") for t in range(LANES)]
        cv_win = [sb([P, N + SPARE], F32, f"cv_win{t}") for t in range(LANES)]
        for t in range(LANES):
            nc.vector.memset(a_win[t][:, H:], 0.0)
        for t in range(LANES):
            nc.vector.memset(ds_win[t][:, N:], 0.0)
        for t in range(LANES):
            nc.vector.memset(cv_win[t][:, N:], 0.0)

        for q in range(4):
            rows = slice(32 * q, 32 * q + 4)
            nc.vector.tensor_copy(xs[rows, :].bitcast(I32), xs_rows[rows, :].bitcast(I32))

        def interleave(copy, dst, src, c0, c1):
            copy(
                dst[:, LANES * c0 : LANES * c1].rearrange("p (c i j) -> p c j i", i=4, j=LANES),
                src[:, :, c0:c1].rearrange("p j (c i) -> p c j i", i=4),
            )

        def quantise(src, name):
            codes = sb([P, 512], U32, name + "_codes")
            scales = sb([P, 512], U8, name + "_scales")
            nc.vector.quantize_mx(out=codes[:].bitcast(FP8X4), scales=scales[:], in_=src[:])
            return codes, scales

        def pick_bytes(idx, name):
            plain = sb([P, S], U8, name + "_plain")
            nc.vector.tensor_copy(plain[:], xs[:].indirect(idx[:]))
            dealt = sb([P, S], U8, name + "_dealt")
            nc.vector.tensor_copy(
                dealt[:].bitcast(I32).rearrange("p (t q r) -> p q t r", t=LANES, r=2),
                plain[:].bitcast(I32).rearrange("p (q t r) -> p q t r", t=LANES, r=2),
            )
            return dealt

        def pick_words(idx, name):
            dealt = sb([P, S], U32, name)
            nc.vector.tensor_copy(
                dealt[:].rearrange("p (t q r) -> p q t r", t=LANES, r=8), xw[:].bitcast(U32).indirect(idx[:])
            )
            return dealt

        def product(out, lhs, t, rhs):
            cols = slice(P * t, P * (t + 1))
            nc.tensor.matmul_mx(
                out=out[:],
                lhsT=lhs[0][:, cols].bitcast(FP8X4),
                lhsT_scale=lhs[1][:, cols],
                rhs=rhs[0][:].bitcast(FP8X4),
                rhs_scale=rhs[1][:],
                start=True,
                stop=True,
            )

        xb_scales = pick_bytes(two_sb, "xb_scales")
        xa_scales = pick_bytes(offs_sb, "xa_scales")
        xb = (pick_words(two_sb, "xb_words"), xb_scales)
        wb_bf = sb([P, LANES * N], BF16, "wb_bf", "xa_words")
        interleave(nc.scalar.copy, wb_bf, wb_raw, 0, N)
        wb_q = quantise(wb_bf, "wb")
        xa = (pick_words(offs_sb, "xa_words"), xa_scales)
        wa_bf = sb([P, LANES * H], BF16, "wa_bf", "wa_bf_then_old0")
        interleave(nc.vector.tensor_copy, wa_bf, wa_raw, 0, H)
        wa_q = quantise(wa_bf, "wa")

        st = sb([P, LANES * H], F32, "st")
        z2_rows = sb([P, LANES, N], BF16, "z2_rows")

        def a_load(t):
            a_ps = bank("ring", f"a_ps{t}")
            product(a_ps, xa, t, wa_q)
            if t in ():
                nc.vector.tensor_scalar(a_win[t][:, 0:H], a_ps[:], gt_abs[:, t : t + 1], None, ALU.mult)
            else:
                nc.scalar.activation(a_win[t][:, 0:H], a_ps[:], ACT.Copy, scale=gt_abs[:, t : t + 1])

        mx = {}

        def a_half(t, h):
            if h == 0:
                mx[t] = sb([P, H], F32, f"mx{t}", "mx3_then_st_n2" if t == 3 else None)
            mb = sb([P, H], F32, f"mb{t}_{h}", f"mb3_{h}_then_st_n2" if t == 3 else None)
            nc.scalar.activation(mb[:], a_win[t][:].indirect(n1_sb[:, 32 * h : 32 * (h + 1)]), ACT.Copy)
            pairs = mb[:].rearrange("p (j m) -> p j m", m=2)
            nc.vector.tensor_tensor(mx[t][:, HALF * h : HALF * (h + 1)], pairs[:, :, 0], pairs[:, :, 1], ALU.max)

        def a_less(t):
            nc.vector.tensor_tensor(st[:, H * t : H * (t + 1)], a_win[t][:, 0:H], mx[t][:], ALU.subtract)

        def a_partner(t, h):
            picked = st[:, H * t : H * (t + 1)].indirect(n2_sb[:, PIECES[h][0] // 16 : PIECES[h][1] // 16])
            if (t, h) in ((3, 0), (3, 1)):
                nc.vector.tensor_copy(st_n2[h][:, t, :], picked)
            else:
                nc.scalar.activation(st_n2[h][:, t, :], picked, ACT.Copy)

        def b_load(t, copy):
            b_ps = bank("ring" if t else "first", f"b_ps{t}")
            product(b_ps, xb, t, wb_q)
            copy(ds_win[t][:, 0:N], b_ps[:])

        less_low = {}

        def b_path(t, old_on_vector):
            b_pick(t, old_on_vector)
            b_put(t)

        def b_pick(t, old_on_vector=False):
            less = sb([P, G], F32, f"less{t}")
            nc.scalar.activation(less[:], ds_win[t][:].indirect(n4_sb[:]), ACT.Copy, scale=-0.5)
            old = sb([P, G], F32, f"old{t}", "wa_bf_then_old0" if t == 0 else None)
            if old_on_vector:
                nc.vector.tensor_copy(old[:], ds_win[t][:].indirect(n3_sb[:]))
            else:
                nc.scalar.activation(old[:], ds_win[t][:].indirect(n3_sb[:]), ACT.Copy)
            low = sb([P, G], F32, f"low{t}", "low01" if t < 2 else None)
            nc.vector.scalar_tensor_tensor(low[:], less[:], -2.0, old[:], ALU.mult, ALU.min)
            less_low[t] = (less, low)

        def b_put(t):
            less, low = less_low[t]
            nc.vector.tensor_tensor(ds_win[t][:].indirect(n3_sb[:]), low[:], less[:], ALU.add)

        def b_weigh(t, on_vector=True):
            if on_vector:
                nc.vector.tensor_scalar(z2_rows[:, t, :], ds_win[t][:, 0:N], gi_signed[:, t : t + 1], None, ALU.mult)
            else:
                nc.scalar.activation(z2_rows[:, t, :], ds_win[t][:, 0:N], ACT.Copy, scale=gi_signed[:, t : t + 1])

        b_load(0, nc.scalar.copy)
        b_load(1, nc.scalar.copy)
        gate_ps = bank("first", "gate_ps")
        nc.tensor.transpose(gate_ps[:, 0:P], gate_rows[:], ident[:])
        gt_step = sb([P, LANES], F32, "gt_step")
        nc.vector.tensor_scalar(gt_step[:], gate_ps[:, 0:LANES], 0.0, 2.0, ALU.is_ge, ALU.mult)
        gt_abs = sb([P, LANES], F32, "gt_abs")
        nc.vector.scalar_tensor_tensor(gt_abs[:], gt_step[:], -1.0, gate_ps[:, 0:LANES], ALU.add, ALU.mult)
        gi_signed = sb([P, LANES], F32, "gi_signed")
        nc.vector.scalar_tensor_tensor(
            gi_signed[:], gt_step[:], -1.0, gate_ps[:, LANES : 2 * LANES], ALU.add, ALU.mult
        )

        b_path(0, True)
        b_path(1, False)
        b_weigh(0)
        for t in range(2):
            a_load(t)
            b_load(t + 2, nc.scalar.copy)
            a_half(t, 0)
            b_weigh(t + 1)
            b_pick(t + 2)
            a_half(t, 1)
            b_put(t + 2)
            a_less(t)
        a_load(2)
        a_load(3)
        a_half(2, 0)
        b_weigh(3)
        a_half(2, 1)
        a_half(3, 0)
        a_less(2)
        a_half(3, 1)
        z2_bf = sb([P, LANES * N], BF16, "z2_bf")
        interleave(nc.vector.tensor_copy, z2_bf, z2_rows, 0, N)
        a_less(3)
        z2_q = quantise(z2_bf, "z2")
        st_n2 = [
            sb([P, LANES, c1 - c0], F32, f"st_n2_{i}", ("mb3_0_then_st_n2", "mx3_then_st_n2", "a_win3", None)[i])
            for i, (c0, c1) in enumerate(PIECES)
        ]

        z_bf = sb([P, LANES * H], BF16, "z_bf")
        for i, (c0, c1) in enumerate(PIECES):
            for t in range(LANES):
                a_partner(t, i)
            ms = slice(c0 // LANES, c1 // LANES)
            nc.vector.tensor_tensor(
                z_bf[:].rearrange("p (u m j) -> p m j u", u=LANES, j=LANES)[:, ms],
                st[:].rearrange("p (j m u) -> p m j u", j=LANES, u=LANES)[:, ms],
                st_n2[i][:].rearrange("p j (m u) -> p m j u", u=LANES),
                ALU.max,
            )
        z_codes = sb([P, 512], U32, "z_codes")
        z_scales = sb([P, 512], U8, "z_scales")
        z_q = (z_codes, z_scales)

        y = [sb([P, LANES, HALF], F32, f"y{h}") for h in range(2)]
        y_rows = out_0.rearrange("(p u) n -> p u n", u=LANES)
        cv_ps = []
        for c0, c1 in ((0, P), (P, H)):
            nc.vector.quantize_mx(
                out=z_codes[:, c0:c1].bitcast(FP8X4), scales=z_scales[:, c0:c1], in_=z_bf[:, LANES * c0 : LANES * c1]
            )
        for u in range(LANES):
            cv_ps.append(bank(f"cv{u}", f"cv_ps{u}"))
            product(cv_ps[u], z_q, u, z2_q)

        st2 = [sb([P, N], F32, f"st2_{u}") for u in range(LANES)]

        def cv_load(u, on_vector):
            if on_vector:
                nc.vector.tensor_scalar(cv_win[u][:, 0:N], cv_ps[u][:], -0.03125, None, ALU.mult)
            else:
                nc.scalar.activation(cv_win[u][:, 0:N], cv_ps[u][:], ACT.Copy, scale=-0.03125)

        def cv_partner(u):
            cv_n5 = sb([P, N], F32, f"cv_n5_{u}")
            nc.scalar.activation(cv_n5[:], cv_win[u][:].indirect(n5_sb[:]), ACT.Copy, scale=-2.0)
            nc.vector.scalar_tensor_tensor(st2[u][:], cv_ps[u][:], 0.0625, cv_n5[:], ALU.mult, ALU.max)

        def finish(u, h, how):
            adder = nc.gpsimd if how in ("sg", "vg") else nc.vector
            cols = slice(HALF * h, HALF * (h + 1))
            picked = st2[u][:].indirect(n6_sb[:, 16 * h : 16 * (h + 1)])
            if how != "fused":
                plain = sb([P, HALF], F32, f"st2_n6_{u}_{h}")
                if how in ("s", "sg"):
                    nc.scalar.activation(plain[:], picked, ACT.Copy)
                else:
                    nc.vector.tensor_copy(plain[:], picked)
                picked = plain[:]
            adder.tensor_tensor(y[h][:, u, :], picked, cv_win[u][:, cols], ALU.add)
            store(u, h)

        y_bf = [sb([P, LANES * HALF], BF16, f"y_bf{h}") for h in range(2)]
        y_codes = sb([P, N], U32, "y_codes")
        y_scales = sb([P, N], U8, "y_scales")
        words_out = out_1[0].rearrange("p n t -> p (n t)").bitcast(I32)

        def planes(h, shares):
            cols = slice(HALF * h, HALF * (h + 1))
            for copy, c0, c1 in shares:
                interleave(copy, y_bf[h], y[h], c0, c1)
            nc.vector.quantize_mx(out=y_codes[:, cols].bitcast(FP8X4), scales=y_scales[:, cols], in_=y_bf[h][:])
            nc.sync.dma_start(words_out[:, cols], y_codes[:, cols].bitcast(I32))

        def store(u, h):
            nc.sync.dma_start(y_rows[:, u, HALF * h : HALF * (h + 1)], y[h][:, u, :])

        cv_load(0, False)
        cv_load(1, True)
        cv_load(2, True)
        cv_load(3, True)
        cv_partner(0)
        finish(0, 0, "fused")
        cv_partner(1)
        finish(1, 0, "fused")
        cv_partner(2)
        finish(0, 1, "fused")
        cv_partner(3)
        finish(2, 0, "s")
        finish(3, 0, "s")
        finish(1, 1, "fused")
        finish(2, 1, "s")
        planes(0, ((nc.scalar.copy, 0, HALF),))
        finish(3, 1, "fused")
        planes(1, ((nc.scalar.copy, 0, 96), (nc.vector.tensor_copy, 96, HALF)))
        for q in range(4):
            (nc.sync, nc.scalar)[q % 2].dma_start(
                out_2[0, 4 * q : 4 * q + 4, :].bitcast(I32), y_scales[32 * q : 32 * q + 4, :].bitcast(I32)
            )
